import numpy as np
import ml_dtypes


def mxq(x, axis, fmt="e4m3"):
    dtype, down = {"e4m3": (ml_dtypes.float8_e4m3fn, 7), "e5m2": (ml_dtypes.float8_e5m2, 14)}[fmt]
    v = np.moveaxis(np.asarray(x, np.float32).astype(ml_dtypes.bfloat16).astype(np.float64), axis, -1)
    blocks = v.reshape(v.shape[:-1] + (-1, 32))
    amax = np.abs(blocks).max(-1, keepdims=True)
    byte = np.maximum(np.where(amax > 0, np.frexp(amax)[1] - 1 + 127, 0) - down, 1)
    scale = np.exp2(byte - 127.0)
    codes = (blocks / scale).astype(np.float32).astype(dtype).astype(np.float64)
    return np.moveaxis((codes * scale).reshape(v.shape), -1, axis)


WIDE = False


def mx_kscale(k):
    if not WIDE:
        return np.ones(k)
    levels = np.array([10, -10, 5, -5, 0])
    if k % 512:
        return np.exp2(np.random.permutation(np.resize(levels, k // 32))).repeat(32)
    a = np.empty((k // 512, 16))
    for p in range(k // 512):
        a[p, :8] = np.random.permutation(np.resize(levels, 8))
        for g in range(8):
            far = levels[np.abs(levels - a[p, g]) >= 10]
            a[p, g + 8] = far[np.random.randint(len(far))]
    return np.exp2(a.ravel()).repeat(32)


def f64(x):
    return np.asarray(x).astype(np.float64)


def striped(idx):
    return np.tile(idx.reshape(-1, 16).T, (8, 1)).astype(np.uint16)


def unstriped(offs):
    return offs[:16].T.reshape(-1).astype(np.int64)


def striped8(idx):
    return np.concatenate([x.reshape(-1, 16).T for x in idx]).astype(np.uint16)


def runs(offs, k):
    lists = np.stack([offs[16 * r : 16 * r + 16].T.reshape(-1) for r in range(8)]).astype(np.int64)
    return lists[np.arange(k) % 512 // 64]


def pack_weight(w):
    k, n = w.shape
    w = f64(np.asarray(w, np.float32).astype(ml_dtypes.bfloat16)).reshape(k // 32, 32, n)
    amax = np.abs(w).max(1)
    byte = np.clip(np.where(amax > 0, np.frexp(amax)[1] - 1 + 127 - 7, 1), 1, 254)
    scaled = (w * np.exp2(127.0 - byte)[:, None, :]).reshape(k, n).astype(np.float32)
    words = np.ascontiguousarray(scaled.reshape(k // 512, 128, 4, n).transpose(0, 1, 3, 2)).astype(ml_dtypes.float8_e4m3fn).view(np.uint8)
    return words, np.ascontiguousarray(byte.astype(np.uint8).reshape(k // 512, 16, n))


def unpack_weight(words, scales):
    g, p, n, _ = words.shape
    vals = np.ascontiguousarray(words).view(ml_dtypes.float8_e4m3fn).astype(np.float64) * np.repeat(np.exp2(scales.astype(np.float64) - 127.0), 8, axis=1)[..., None]
    return vals.transpose(0, 1, 3, 2).reshape(g * 512, n)


E2M1 = np.array([0.0, 0.5, 1.0, 1.5, 2.0, 3.0, 4.0, 6.0, -0.0, -0.5, -1.0, -1.5, -2.0, -3.0, -4.0, -6.0])


def pack_fp4(w):
    k, n = w.shape
    w = f64(np.asarray(w, np.float32).astype(ml_dtypes.bfloat16)).reshape(k // 32, 32, n)
    amax = np.abs(w).max(1)
    mant, ex = np.frexp(amax / 6.0)
    byte = np.clip(np.where(amax > 0, np.where(mant > 0.5, ex, ex - 1) + 127, 1), 1, 254)
    scaled = (w * np.exp2(127.0 - byte)[:, None, :]).reshape(k, n).astype(np.float32)
    c = np.ascontiguousarray(scaled.reshape(k // 512, 128, 4, n).transpose(0, 1, 3, 2)).astype(ml_dtypes.float4_e2m1fn).view(np.uint8) & 0xF
    words = (c[..., 0::2] | (c[..., 1::2] << 4)).reshape(k // 512, 128, 2 * n)
    return np.ascontiguousarray(words), np.ascontiguousarray(byte.astype(np.uint8).reshape(k // 512, 16, n))


def unpack_fp4(words, scales):
    g, _, n = scales.shape
    words = np.ascontiguousarray(words).reshape(g, 128, n, 2)
    nib = np.empty((g, 128, n, 4), np.uint8)
    nib[..., 0::2] = words & 0xF
    nib[..., 1::2] = words >> 4
    vals = E2M1[nib] * np.repeat(np.exp2(scales.astype(np.float64) - 127.0), 8, axis=1)[..., None]
    return vals.transpose(0, 1, 3, 2).reshape(g * 512, n)


def sigmoid(v):
    return 1.0 / (1.0 + np.exp(-np.maximum(v, -700.0)))

def planes(y):
    n, m = y.shape
    v = y.astype(np.float32).astype(ml_dtypes.bfloat16).astype(np.float64).reshape(n // 32, 32, m)
    top = np.abs(v).max(1)
    byte = np.clip(np.where(top > 0, np.frexp(top)[1] - 1 + 127 - 7, 1), 1, 254)
    codes = (v * np.exp2(127.0 - byte)[:, None, :]).reshape(n, m).astype(np.float32).astype(ml_dtypes.float8_e4m3fn).view(np.uint8)
    words = codes.reshape(n // 512, 128, 4, m).transpose(0, 1, 3, 2)
    return np.ascontiguousarray(words), np.ascontiguousarray(byte.astype(np.uint8).reshape(n // 512, 16, m))


K, T, S, H, W, C, G = 512, 1024, 512, 512, 2048, 512, 2048


def setup_inputs():
    n = np.random.standard_normal
    s = mx_kscale(K)[:, None]
    packed_xT = pack_weight(n((K, T)) * s)
    packed_w1 = pack_fp4(n((K, H)) / np.sqrt(K) / s)
    packed_dT = pack_weight(n((K, G)) / s)
    return {
        "x_words": packed_xT[0],
        "x_scales": packed_xT[1],
        "w1_words": packed_w1[0],
        "w1_scales": packed_w1[1],
        "gs": (np.random.uniform(0.5, 1.5, (K, 1)) / s).astype(np.float32),
        "gk": (np.random.uniform(0.5, 1.5, (K, 1)) * s).astype(np.float32),
        "d_words": packed_dT[0],
        "d_scales": packed_dT[1],
        "offs": striped(np.random.permutation(T)[:S]),
        "n1": striped(np.random.randint(0, S, W)),
        "n2": striped8(np.stack([np.random.permutation(S) for _ in range(8)])),
        "n3": striped8(np.stack([np.random.permutation(S) for _ in range(8)])),
        "cand": striped(np.random.permutation(T)[:C]),
        "k1": striped8(np.random.randint(0, G, (8, H))),
        "n4": striped(np.random.permutation(S)),
        "n5": striped(np.random.permutation(S)),
    }


def reference(x_words, x_scales, w1_words, w1_scales, gs, gk, d_words, d_scales, offs, n1, n2, n3, cand, k1, n4, n5):
    x_cand = unpack_weight(x_words, x_scales)[:, unstriped(cand)]
    xq = unpack_weight(x_words, x_scales)[:, unstriped(offs)]
    y = unpack_fp4(w1_words, w1_scales).T @ xq
    ex = np.exp(y)
    mb = ex[:, unstriped(n1)]
    ms = mb.reshape(H, S, 4).sum(axis=2)
    z = f64(gs) * (np.log(ms + ex) - y)
    a = 0.0625 * ((x_cand.T @ mxq(z, 0, "e4m3")))
    d_k1 = unpack_weight(d_words, d_scales)[np.arange(K)[:, None], runs(k1, K)]
    z2 = f64(gk) * (y * (sigmoid(y[np.arange(H)[:, None], runs(n2, H)] - (y[np.arange(H)[:, None], runs(n3, H)]))))
    b = 0.0625 * ((d_k1.T @ mxq(z2, 0, "e4m3")))
    out_0 = (a + a[:, unstriped(n4)]) * (sigmoid(b + b[:, unstriped(n5)]))
    return (out_0,) + planes(out_0)

@@ -1,0 +1,261 @@
+from contextlib import ExitStack
+
+import concourse.mybir as mybir
+
+F32 = mybir.dt.float32
+BF16 = mybir.dt.bfloat16
+I32 = mybir.dt.int32
+U32 = mybir.dt.uint32
+U16 = mybir.dt.uint16
+U8 = mybir.dt.uint8
+FP8X4 = mybir.dt.float8_e4m3fn_x4
+FP4X4 = mybir.dt.float4_e2m1fn_x4
+ACT = mybir.ActivationFunctionType
+ALU = mybir.AluOpType
+
+P = 128
+PACK = 4
+S = 512
+T = 1024
+G = 2048
+MEMBERS = 4
+SPARE = 16
+CHUNKS = (256, 256)
+
+FLOPS = 3 * 2 * 512 * 512 * 512
+
+
+def tile_picked_cdkeytriebglsecmp_none_po_kernel(
+    tc, x_words, x_scales, w1_words, w1_scales, gs, gk, d_words, d_scales,
+    offs, n1, n2, n3, cand, k1, n4, n5, out_0, out_1, out_2,
+):
+    nc = tc.nc
+    with ExitStack() as ctx:
+        lists = ctx.enter_context(tc.tile_pool(name="lists", bufs=1))
+        keep = ctx.enter_context(tc.tile_pool(name="keep", bufs=1))
+        psum = ctx.enter_context(tc.psum_pool(name="psum", bufs=1))
+
+        def load_list(src, name):
+            tile = lists.tile([P, src.shape[1]], U16, name=name)
+            nc.sync.dma_start(tile[:], src)
+            return tile
+
+        def sb(shape, dtype, name, tag=None):
+            return keep.tile(shape, dtype, name=name, tag=tag or name, align_bytes=64)
+
+        def zeroed_bytes(width, name):
+            tile = sb([P, width], U8, name)
+            nc.vector.memset(tile[:].bitcast(I32), 0)
+            return tile
+
+        def load_scale_rows(queue, tile, scales):
+            for q in range(4):
+                queue.dma_start(
+                    tile[32 * q : 32 * q + 4, :].bitcast(I32),
+                    scales[0, 4 * q : 4 * q + 4, :].bitcast(I32),
+                )
+
+        def deal(dst, src):
+            nc.vector.tensor_copy(
+                dst[:].rearrange("p (t m) -> p t m", t=PACK),
+                src[:].rearrange("p (m t) -> p t m", t=PACK),
+            )
+
+        def gather(dst, window, offsets):
+            nc.scalar.activation(dst, window[:].indirect(offsets), ACT.Copy)
+
+        def quantize(values, codes, scales, staged):
+            nc.vector.tensor_copy(staged.rearrange("p (n t) -> p n t", t=PACK), values.rearrange("p t n -> p n t"))
+            nc.vector.quantize_mx(out=codes.bitcast(FP8X4), scales=scales, in_=staged)
+
+        xs = zeroed_bytes(T, "xs")
+        ws = zeroed_bytes(S, "ws")
+        offs_sb = load_list(offs, "offs_sb")
+        ww = sb([P, 2 * S], U8, "ww")
+        nc.sync.dma_start(ww[:].bitcast(I32), w1_words[0].bitcast(I32))
+        xw = sb([P, T], U32, "xw")
+        nc.sync.dma_start(xw[:].bitcast(I32), x_words[0].rearrange("p n t -> p (n t)").bitcast(I32))
+        load_scale_rows(nc.scalar, xs, x_scales)
+        load_scale_rows(nc.sync, ws, w1_scales)
+        n1_sb = load_list(n1, "n1_sb")
+        gs_sb = sb([P, PACK], F32, "gs_sb")
+        nc.sync.dma_start(gs_sb[:], gs.rearrange("(p t) o -> p (t o)", t=PACK))
+        n2_sb = load_list(n2, "n2_sb")
+        n3_sb = load_list(n3, "n3_sb")
+        gk_sb = sb([P, PACK], F32, "gk_sb")
+        nc.sync.dma_start(gk_sb[:], gk.rearrange("(p t) o -> p (t o)", t=PACK))
+        k1_sb = load_list(k1, "k1_sb")
+        dw = sb([P, G], U32, "dw")
+        nc.sync.dma_start(dw[:].bitcast(I32), d_words[0].rearrange("p n t -> p (n t)").bitcast(I32))
+        ds = zeroed_bytes(G, "ds")
+        for e in range(2):
+            nc.sync.dma_start(ds[e:P:16, :].bitcast(I32), d_scales[0, e:16:2, :].bitcast(I32))
+        cand_sb = load_list(cand, "cand_sb")
+        n5_sb = load_list(n5, "n5_sb")
+        n4_sb = load_list(n4, "n4_sb")
+
+        ex = [sb([P, S + SPARE], F32, "ex%d" % t) for t in range(PACK)]
+        a_half = [sb([P, S + SPARE], F32, "a_half%d" % t) for t in range(PACK)]
+        b = [sb([P, S + SPARE], F32, "b%d" % t) for t in range(PACK)]
+        for window in ex + b + a_half:
+            nc.vector.memset(window[:, S:], 0.0)
+        key_s = zeroed_bytes(S, "key_s")
+
+        w_dealt = sb([P, 2 * S], U8, "w_dealt")
+        nc.vector.tensor_copy(
+            w_dealt[:].rearrange("p (t m b) -> p t m b", t=PACK, b=2),
+            ww[:].rearrange("p (m t b) -> p t m b", t=PACK, b=2),
+        )
+        xq_s = sb([P, S], U8, "xq_s")
+        nc.vector.tensor_copy(xq_s[:], xs[:].indirect(offs_sb[:]))
+        xq_w = sb([P, S], U32, "xq_w")
+        nc.vector.tensor_copy(xq_w[:], xw[:].indirect(offs_sb[:]))
+        ws_dealt = sb([P, S], U8, "ws_dealt")
+        deal(ws_dealt, ws)
+
+        y_ps = []
+        for t in range(PACK):
+            bank = psum.tile([P, S], F32, name="y_ps%d" % t, tag="bank%d" % t)
+            nc.tensor.matmul_mx(
+                out=bank[:],
+                lhsT=w_dealt[:, 2 * P * t : 2 * P * (t + 1)].bitcast(FP4X4),
+                lhsT_scale=ws_dealt[:, P * t : P * (t + 1)],
+                rhs=xq_w[:].bitcast(FP8X4),
+                rhs_scale=xq_s[:],
+                start=True,
+                stop=True,
+            )
+            y_ps.append(bank)
+
+        y = [sb([P, 2 * S], F32, "y%d" % t) for t in range(PACK)]
+        y_gk = sb([P, PACK, S], F32, "y_gk")
+        for t in range(PACK):
+            nc.scalar.activation(ex[t][:, :S], y_ps[t][:], ACT.Exp)
+            nc.vector.tensor_copy(y[t][:, :S], y_ps[t][:])
+            nc.vector.tensor_scalar(y[t][:, S:], y[t][:, :S], gs_sb[:, t : t + 1], None, ALU.mult)
+
+        key_w_raw = sb([P, S], U32, "key_w_raw")
+        nc.vector.tensor_copy(key_w_raw[:], dw[:].indirect(k1_sb[:]))
+        key_s_raw = sb([P, S], U8, "key_s_raw")
+        nc.vector.tensor_copy(key_s_raw[:], ds[:].indirect(k1_sb[:]))
+        key_s_dealt = sb([P, S], U8, "key_s_dealt")
+        deal(key_s_dealt, key_s_raw)
+        for h in range(2):
+            for e in range(2):
+                nc.sync.dma_start(
+                    key_s[2 * h + e : P : 32, :].bitcast(I32),
+                    key_s_dealt[16 * h + e : P : 32, :].bitcast(I32),
+                )
+        key_w = sb([P, S], U32, "key_w")
+        deal(key_w, key_w_raw)
+
+        y2 = sb([P, PACK, S], F32, "y_n2")
+        y3 = sb([P, PACK, S], F32, "y_n3")
+        diff = sb([P, PACK, S], F32, "diff")
+        for t in range(PACK):
+            gather(y2[:, t, :], y[t], n2_sb[:])
+            gather(y3[:, t, :], y[t], n3_sb[:])
+            nc.vector.tensor_scalar(y_gk[:, t, :], y[t][:, :S], gk_sb[:, t : t + 1], 0.5, ALU.mult, ALU.mult)
+            nc.vector.tensor_tensor(diff[:, t, :], y2[:, t, :], y3[:, t, :], ALU.subtract)
+        th1 = sb([P, PACK, S], F32, "th1", tag="y_n2")
+        nc.scalar.activation(th1[:], diff[:], ACT.Tanh, scale=0.5)
+
+        cand_w_raw = sb([P, S], U32, "cand_w_raw")
+        nc.vector.tensor_copy(cand_w_raw[:], xw[:].indirect(cand_sb[:]))
+        cand_s_raw = sb([P, S], U8, "cand_s_raw")
+        nc.vector.tensor_copy(cand_s_raw[:], xs[:].indirect(cand_sb[:]))
+        cand_w = sb([P, S], U32, "cand_w")
+        deal(cand_w, cand_w_raw)
+        cand_s = sb([P, S], U8, "cand_s")
+        deal(cand_s, cand_s_raw)
+
+        def product(stat_w, stat_s, mov_w, mov_s, first_bank, dst, factor, name):
+            for t in range(PACK):
+                bank = psum.tile([P, S], F32, name="%s_ps%d" % (name, t), tag="bank%d" % (first_bank + t))
+                nc.tensor.matmul_mx(
+                    out=bank[:],
+                    lhsT=stat_w[:, P * t : P * (t + 1)].bitcast(FP8X4),
+                    lhsT_scale=stat_s[:, P * t : P * (t + 1)],
+                    rhs=mov_w[:].bitcast(FP8X4),
+                    rhs_scale=mov_s[:],
+                    start=True,
+                    stop=True,
+                )
+                nc.vector.tensor_scalar(dst[t][:, :S], bank[:], factor, None, ALU.mult)
+
+        members = [sb([P, MEMBERS * S], F32, "members%d" % t) for t in range(PACK)]
+        pairs = sb([P, 2 * S], F32, "pairs")
+        total = sb([P, PACK, S], F32, "total")
+
+        def member_sums(t):
+            for c in range(MEMBERS):
+                gather(members[t][:, S * c : S * (c + 1)], ex[t], n1_sb[:, 32 * c : 32 * (c + 1)])
+            view = members[t][:].rearrange("p (j h e) -> p j h e", h=2, e=2)
+            pv = pairs[:].rearrange("p (j e) -> p j e", e=2)
+            nc.vector.tensor_tensor(pv, view[:, :, 0, :], view[:, :, 1, :], ALU.add)
+            nc.vector.tensor_tensor(total[:, t, :], pv[:, :, 0], pv[:, :, 1], ALU.add)
+            nc.vector.tensor_tensor(total[:, t, :], total[:, t, :], ex[t][:, :S], ALU.add)
+
+        z2 = sb([P, PACK, S], F32, "z2", tag="y_n3")
+        nc.vector.scalar_tensor_tensor(z2[:], th1[:], 1.0, y_gk[:], ALU.add, ALU.mult)
+        z2_bf = sb([P, PACK * S], BF16, "z2_bf")
+        z2_w = sb([P, S], U32, "z2_w")
+        z2_s = sb([P, S], U8, "z2_s")
+        member_sums(0)
+        quantize(z2[:], z2_w[:], z2_s[:], z2_bf[:])
+        member_sums(1)
+        product(key_w, key_s, z2_w, z2_s, PACK, b, 0.0625, "b")
+        member_sums(2)
+        member_sums(3)
+
+        logs = sb([P, PACK, S], F32, "logs")
+        nc.scalar.activation(logs[:, : PACK - 1, :], total[:, : PACK - 1, :], ACT.Ln)
+        nc.scalar.activation(logs[:, PACK - 1, :], total[:, PACK - 1, :], ACT.Ln)
+        z = sb([P, PACK, S], F32, "z", tag="diff")
+        for t in range(PACK):
+            nc.vector.scalar_tensor_tensor(
+                z[:, t, :], logs[:, t, :], gs_sb[:, t : t + 1], y[t][:, S:], ALU.mult, ALU.subtract
+            )
+        z_bf = sb([P, PACK * S], BF16, "z_bf")
+        z_w = sb([P, S], U32, "z_w")
+        z_s = sb([P, S], U8, "z_s")
+        quantize(z[:], z_w[:], z_s[:], z_bf[:])
+
+        starts = [sum(CHUNKS[:c]) for c in range(len(CHUNKS))]
+        b5 = sb([P, PACK, S], F32, "b5", tag="total")
+        logit = [sb([P, PACK, n], F32, "logit%d" % c) for c, n in enumerate(CHUNKS)]
+        for c, n in enumerate(CHUNKS):
+            c0 = starts[c]
+            for t in range(PACK):
+                gather(b5[:, t, c0 : c0 + n], b[t], n5_sb[:, c0 // 16 : (c0 + n) // 16])
+        product(cand_w, cand_s, z_w, z_s, 0, a_half, 0.03125, "a")
+        for c, n in enumerate(CHUNKS):
+            c0 = starts[c]
+            for t in range(PACK):
+                nc.vector.tensor_tensor(logit[c][:, t, :], b5[:, t, c0 : c0 + n], b[t][:, c0 : c0 + n], ALU.add)
+
+        out_rows = out_0.rearrange("(p t) j -> p t j", t=PACK)
+        out_words = out_1[0].rearrange("p n t -> p (n t)").bitcast(I32)
+        o_w = sb([P, S], U32, "o_w")
+        o_s = sb([P, S], U8, "o_s")
+        for c, n in enumerate(CHUNKS):
+            c0 = starts[c]
+            th2 = sb([P, PACK, n], F32, "th2_%d" % c)
+            nc.scalar.activation(th2[:], logit[c][:], ACT.Tanh, scale=0.5)
+            a4 = sb([P, PACK, n], F32, "a4_%d" % c, tag="logit%d" % c)
+            both = sb([P, PACK, n], F32, "both%d" % c)
+            res = sb([P, PACK, n], F32, "res%d" % c)
+            for t in range(PACK):
+                gather(a4[:, t, :], a_half[t], n4_sb[:, c0 // 16 : (c0 + n) // 16])
+                nc.vector.tensor_tensor(both[:, t, :], a4[:, t, :], a_half[t][:, c0 : c0 + n], ALU.add)
+                nc.vector.scalar_tensor_tensor(res[:, t, :], th2[:, t, :], 1.0, both[:, t, :], ALU.add, ALU.mult)
+                if t % 2 == 1:
+                    nc.sync.dma_start(out_rows[:, t - 1 : t + 1, c0 : c0 + n], res[:, t - 1 : t + 1, :])
+            o_bf = sb([P, PACK * n], BF16, "o_bf%d" % c)
+            quantize(res[:], o_w[:, c0 : c0 + n], o_s[:, c0 : c0 + n], o_bf[:])
+            nc.sync.dma_start(out_words[:, c0 : c0 + n], o_w[:, c0 : c0 + n].bitcast(I32))
+        for q in range(4):
+            queue = nc.scalar if q % 2 == 0 else nc.sync
+            queue.dma_start(
+                out_2[0, 4 * q : 4 * q + 4, :].bitcast(I32), o_s[32 * q : 32 * q + 4, :].bitcast(I32)
+            )

@@ -1,6 +1,7 @@
 from contextlib import ExitStack
 
 import concourse.mybir as mybir
+from concourse.masks import make_identity
 
 F32 = mybir.dt.float32
 BF16 = mybir.dt.bfloat16
@@ -20,7 +21,8 @@ T = 1024
 G = 2048
 MEMBERS = 4
 SPARE = 16
-CHUNKS = (256, 256)
+H = S // 2
+OUT_CHUNKS = (((0, 256),), ((256, 128), (384, 128)))
 
 FLOPS = 3 * 2 * 512 * 512 * 512
 
@@ -48,11 +50,12 @@ def tile_picked_cdkeytriebglsecmp_none_po_kernel(
             nc.vector.memset(tile[:].bitcast(I32), 0)
             return tile
 
-        def load_scale_rows(queue, tile, scales):
-            for q in range(4):
+        def load_scale_rows(queue, tile, scales, quadrants):
+            for q in quadrants:
+                rows = scales[0, 4 * q : 4 * q + 4, :].bitcast(I32)
                 queue.dma_start(
-                    tile[32 * q : 32 * q + 4, :].bitcast(I32),
-                    scales[0, 4 * q : 4 * q + 4, :].bitcast(I32),
+                    tile[32 * q : 32 * q + 32, :].bitcast(I32),
+                    rows.unsqueeze(0).to_broadcast([8, 4, rows.shape[1]]),
                 )
 
         def deal(dst, src):
@@ -65,18 +68,22 @@ def tile_picked_cdkeytriebglsecmp_none_po_kernel(
             nc.scalar.activation(dst, window[:].indirect(offsets), ACT.Copy)
 
         def quantize(values, codes, scales, staged):
-            nc.vector.tensor_copy(staged.rearrange("p (n t) -> p n t", t=PACK), values.rearrange("p t n -> p n t"))
+            nc.vector.tensor_copy(
+                staged.rearrange("p (c i t) -> p c t i", i=4, t=PACK),
+                values.rearrange("p t (c i) -> p c t i", i=4),
+            )
             nc.vector.quantize_mx(out=codes.bitcast(FP8X4), scales=scales, in_=staged)
 
-        xs = zeroed_bytes(T, "xs")
-        ws = zeroed_bytes(S, "ws")
+        xs = sb([P, T], U8, "xs")
+        ws = sb([P, S], U8, "ws")
         offs_sb = load_list(offs, "offs_sb")
-        ww = sb([P, 2 * S], U8, "ww")
-        nc.sync.dma_start(ww[:].bitcast(I32), w1_words[0].bitcast(I32))
+        load_scale_rows(nc.sync, xs, x_scales, (0, 1))
+        load_scale_rows(nc.scalar, xs, x_scales, (2, 3))
         xw = sb([P, T], U32, "xw")
         nc.sync.dma_start(xw[:].bitcast(I32), x_words[0].rearrange("p n t -> p (n t)").bitcast(I32))
-        load_scale_rows(nc.scalar, xs, x_scales)
-        load_scale_rows(nc.sync, ws, w1_scales)
+        ww = sb([P, 2 * S], U8, "ww")
+        nc.sync.dma_start(ww[:].bitcast(I32), w1_words[0].bitcast(I32))
+        load_scale_rows(nc.sync, ws, w1_scales, (0, 1, 2, 3))
         n1_sb = load_list(n1, "n1_sb")
         gs_sb = sb([P, PACK], F32, "gs_sb")
         nc.sync.dma_start(gs_sb[:], gs.rearrange("(p t) o -> p (t o)", t=PACK))
@@ -94,49 +101,85 @@ def tile_picked_cdkeytriebglsecmp_none_po_kernel(
         n5_sb = load_list(n5, "n5_sb")
         n4_sb = load_list(n4, "n4_sb")
 
-        ex = [sb([P, S + SPARE], F32, "ex%d" % t) for t in range(PACK)]
-        a_half = [sb([P, S + SPARE], F32, "a_half%d" % t) for t in range(PACK)]
+        ex = [sb([P, MEMBERS * S + SPARE], F32, "ex%d" % t) for t in range(PACK)]
+        a_half = [sb([P, S + (S if t < 2 else SPARE)], F32, "a_half%d" % t) for t in range(PACK)]
         b = [sb([P, S + SPARE], F32, "b%d" % t) for t in range(PACK)]
-        for window in ex + b + a_half:
-            nc.vector.memset(window[:, S:], 0.0)
         key_s = zeroed_bytes(S, "key_s")
+        ident = sb([P, P], F32, "ident")
+        make_identity(nc, ident[:])
 
-        w_dealt = sb([P, 2 * S], U8, "w_dealt")
-        nc.vector.tensor_copy(
-            w_dealt[:].rearrange("p (t m b) -> p t m b", t=PACK, b=2),
-            ww[:].rearrange("p (m t b) -> p t m b", t=PACK, b=2),
-        )
+        w_first = sb([P, 2 * P], U8, "w_first")
+        ws_first = sb([P, P], U8, "ws_first")
+        ww_by_t = ww[:].rearrange("p (m t b) -> p t m b", t=PACK, b=2)
+        ws_by_t = ws[:].rearrange("p (m t) -> p t m", t=PACK)
+        nc.vector.tensor_copy(w_first[:].rearrange("p (m b) -> p m b", b=2), ww_by_t[:, 0])
         xq_s = sb([P, S], U8, "xq_s")
         nc.vector.tensor_copy(xq_s[:], xs[:].indirect(offs_sb[:]))
         xq_w = sb([P, S], U32, "xq_w")
-        nc.vector.tensor_copy(xq_w[:], xw[:].indirect(offs_sb[:]))
-        ws_dealt = sb([P, S], U8, "ws_dealt")
-        deal(ws_dealt, ws)
-
-        y_ps = []
-        for t in range(PACK):
-            bank = psum.tile([P, S], F32, name="y_ps%d" % t, tag="bank%d" % t)
-            nc.tensor.matmul_mx(
-                out=bank[:],
-                lhsT=w_dealt[:, 2 * P * t : 2 * P * (t + 1)].bitcast(FP4X4),
-                lhsT_scale=ws_dealt[:, P * t : P * (t + 1)],
-                rhs=xq_w[:].bitcast(FP8X4),
-                rhs_scale=xq_s[:],
-                start=True,
-                stop=True,
-            )
-            y_ps.append(bank)
+        for h in range(2):
+            nc.vector.tensor_copy(xq_w[:, H * h : H * (h + 1)], xw[:].indirect(offs_sb[:, 16 * h : 16 * (h + 1)]))
+            if h == 0:
+                nc.vector.tensor_copy(ws_first[:], ws_by_t[:, 0])
 
         y = [sb([P, 2 * S], F32, "y%d" % t) for t in range(PACK)]
         y_gk = sb([P, PACK, S], F32, "y_gk")
+
+        def project(t, lhs_w, lhs_s, cols, bank_no):
+            bank = psum.tile([P, cols.stop - cols.start], F32, name="y_ps%d" % bank_no, tag="bank%d" % bank_no)
+            nc.tensor.matmul_mx(
+                out=bank[:],
+                lhsT=lhs_w.bitcast(FP4X4),
+                lhsT_scale=lhs_s,
+                rhs=xq_w[:, cols].bitcast(FP8X4),
+                rhs_scale=xq_s[:, cols],
+                start=True,
+                stop=True,
+            )
+            return bank
+
+        halves = [project(0, w_first[:], ws_first[:], slice(H * h, H * (h + 1)), PACK * h) for h in range(2)]
+        for h in range(2):
+            nc.scalar.activation(ex[0][:, H * h : H * (h + 1)], halves[h][:], ACT.Exp)
+        ws_rest = sb([P, (PACK - 1) * P], U8, "ws_rest")
+        nc.vector.tensor_copy(ws_rest[:].rearrange("p (t m) -> p t m", t=PACK - 1), ws_by_t[:, 1:])
+        w_rest = sb([P, (PACK - 1) * 2 * P], U8, "w_rest", tag="ws")
+        nc.vector.tensor_copy(w_rest[:].rearrange("p (t m b) -> p t m b", t=PACK - 1, b=2), ww_by_t[:, 1:])
+        y_ps = [None] + [
+            project(t, w_rest[:, 2 * P * (t - 1) : 2 * P * t], ws_rest[:, P * (t - 1) : P * t], slice(0, S), t)
+            for t in range(1, PACK)
+        ]
+        members = [sb([P, MEMBERS * S], F32, "members%d" % t) for t in range(PACK)]
+        pairs = sb([P, 2 * S], F32, "pairs")
+        total = sb([P, PACK, S], F32, "total")
+
+        def fetch_members(t, pieces=1):
+            n = MEMBERS * S // pieces
+            for c in range(pieces):
+                gather(members[t][:, n * c : n * (c + 1)], ex[t], n1_sb[:, n * c // 16 : n * (c + 1) // 16])
+
+        def member_sums(t, pieces=1):
+            n = S // pieces
+            view = members[t][:].rearrange("p (j h e) -> p j h e", h=2, e=2)
+            pv = pairs[:].rearrange("p (j e) -> p j e", e=2)
+            for c in range(pieces):
+                js = slice(n * c, n * (c + 1))
+                nc.vector.tensor_tensor(pv[:, js], view[:, js, 0, :], view[:, js, 1, :], ALU.add)
+                nc.vector.tensor_tensor(total[:, t, js], pv[:, js, 0], pv[:, js, 1], ALU.add)
+                nc.vector.tensor_tensor(total[:, t, js], total[:, t, js], ex[t][:, js], ALU.add)
+
+        fetch_members(0)
         for t in range(PACK):
-            nc.scalar.activation(ex[t][:, :S], y_ps[t][:], ACT.Exp)
-            nc.vector.tensor_copy(y[t][:, :S], y_ps[t][:])
+            if t == 0:
+                for h in range(2):
+                    nc.vector.tensor_copy(y[0][:, H * h : H * (h + 1)], halves[h][:])
+            else:
+                nc.scalar.activation(ex[t][:, :S], y_ps[t][:], ACT.Exp)
+                nc.vector.tensor_copy(y[t][:, :S], y_ps[t][:])
             nc.vector.tensor_scalar(y[t][:, S:], y[t][:, :S], gs_sb[:, t : t + 1], None, ALU.mult)
 
-        key_w_raw = sb([P, S], U32, "key_w_raw")
+        key_w_raw = sb([P, S], U32, "key_w_raw", tag="ww")
         nc.vector.tensor_copy(key_w_raw[:], dw[:].indirect(k1_sb[:]))
-        key_s_raw = sb([P, S], U8, "key_s_raw")
+        key_s_raw = sb([P, S], U8, "key_s_raw", tag="ws")
         nc.vector.tensor_copy(key_s_raw[:], ds[:].indirect(k1_sb[:]))
         key_s_dealt = sb([P, S], U8, "key_s_dealt")
         deal(key_s_dealt, key_s_raw)
@@ -157,12 +200,13 @@ def tile_picked_cdkeytriebglsecmp_none_po_kernel(
             gather(y3[:, t, :], y[t], n3_sb[:])
             nc.vector.tensor_scalar(y_gk[:, t, :], y[t][:, :S], gk_sb[:, t : t + 1], 0.5, ALU.mult, ALU.mult)
             nc.vector.tensor_tensor(diff[:, t, :], y2[:, t, :], y3[:, t, :], ALU.subtract)
+        member_sums(0)
         th1 = sb([P, PACK, S], F32, "th1", tag="y_n2")
         nc.scalar.activation(th1[:], diff[:], ACT.Tanh, scale=0.5)
 
-        cand_w_raw = sb([P, S], U32, "cand_w_raw")
+        cand_w_raw = sb([P, S], U32, "cand_w_raw", tag="ww")
         nc.vector.tensor_copy(cand_w_raw[:], xw[:].indirect(cand_sb[:]))
-        cand_s_raw = sb([P, S], U8, "cand_s_raw")
+        cand_s_raw = sb([P, S], U8, "cand_s_raw", tag="ws")
         nc.vector.tensor_copy(cand_s_raw[:], xs[:].indirect(cand_sb[:]))
         cand_w = sb([P, S], U32, "cand_w")
         deal(cand_w, cand_w_raw)
@@ -183,30 +227,19 @@ def tile_picked_cdkeytriebglsecmp_none_po_kernel(
                 )
                 nc.vector.tensor_scalar(dst[t][:, :S], bank[:], factor, None, ALU.mult)
 
-        members = [sb([P, MEMBERS * S], F32, "members%d" % t) for t in range(PACK)]
-        pairs = sb([P, 2 * S], F32, "pairs")
-        total = sb([P, PACK, S], F32, "total")
-
-        def member_sums(t):
-            for c in range(MEMBERS):
-                gather(members[t][:, S * c : S * (c + 1)], ex[t], n1_sb[:, 32 * c : 32 * (c + 1)])
-            view = members[t][:].rearrange("p (j h e) -> p j h e", h=2, e=2)
-            pv = pairs[:].rearrange("p (j e) -> p j e", e=2)
-            nc.vector.tensor_tensor(pv, view[:, :, 0, :], view[:, :, 1, :], ALU.add)
-            nc.vector.tensor_tensor(total[:, t, :], pv[:, :, 0], pv[:, :, 1], ALU.add)
-            nc.vector.tensor_tensor(total[:, t, :], total[:, t, :], ex[t][:, :S], ALU.add)
-
         z2 = sb([P, PACK, S], F32, "z2", tag="y_n3")
         nc.vector.scalar_tensor_tensor(z2[:], th1[:], 1.0, y_gk[:], ALU.add, ALU.mult)
         z2_bf = sb([P, PACK * S], BF16, "z2_bf")
         z2_w = sb([P, S], U32, "z2_w")
         z2_s = sb([P, S], U8, "z2_s")
-        member_sums(0)
         quantize(z2[:], z2_w[:], z2_s[:], z2_bf[:])
+        fetch_members(1)
         member_sums(1)
         product(key_w, key_s, z2_w, z2_s, PACK, b, 0.0625, "b")
+        fetch_members(2)
         member_sums(2)
-        member_sums(3)
+        fetch_members(3, 2)
+        member_sums(3, 2)
 
         logs = sb([P, PACK, S], F32, "logs")
         nc.scalar.activation(logs[:, : PACK - 1, :], total[:, : PACK - 1, :], ACT.Ln)
@@ -221,39 +254,59 @@ def tile_picked_cdkeytriebglsecmp_none_po_kernel(
         z_s = sb([P, S], U8, "z_s")
         quantize(z[:], z_w[:], z_s[:], z_bf[:])
 
-        starts = [sum(CHUNKS[:c]) for c in range(len(CHUNKS))]
         b5 = sb([P, PACK, S], F32, "b5", tag="total")
-        logit = [sb([P, PACK, n], F32, "logit%d" % c) for c, n in enumerate(CHUNKS)]
-        for c, n in enumerate(CHUNKS):
-            c0 = starts[c]
-            for t in range(PACK):
-                gather(b5[:, t, c0 : c0 + n], b[t], n5_sb[:, c0 // 16 : (c0 + n) // 16])
+        for t in range(PACK):
+            gather(b5[:, t, :], b[t], n5_sb[:])
         product(cand_w, cand_s, z_w, z_s, 0, a_half, 0.03125, "a")
-        for c, n in enumerate(CHUNKS):
-            c0 = starts[c]
-            for t in range(PACK):
-                nc.vector.tensor_tensor(logit[c][:, t, :], b5[:, t, c0 : c0 + n], b[t][:, c0 : c0 + n], ALU.add)
+        logit_bank = ((4, 0), (1, 2))
+        logit_ps = {}
+        for h in range(2):
+            for u in range(2):
+                bank = psum.tile([P, 2, 2, P], F32, name="logit_ps%d%d" % (h, u), tag="bank%d" % logit_bank[h][u])
+                for tt in range(2):
+                    t = 2 * u + tt
+                    for jb in range(2):
+                        js = slice(H * h + P * jb, H * h + P * (jb + 1))
+                        for i, term in enumerate((b[t][:, js], b5[:, t, js])):
+                            nc.tensor.matmul(
+                                bank[:, tt, jb, :], term, ident[:], start=(i == 0), stop=(i == 1), is_transpose=True
+                            )
+                logit_ps[h, u] = bank
 
         out_rows = out_0.rearrange("(p t) j -> p t j", t=PACK)
         out_words = out_1[0].rearrange("p n t -> p (n t)").bitcast(I32)
         o_w = sb([P, S], U32, "o_w")
         o_s = sb([P, S], U8, "o_s")
-        for c, n in enumerate(CHUNKS):
-            c0 = starts[c]
-            th2 = sb([P, PACK, n], F32, "th2_%d" % c)
-            nc.scalar.activation(th2[:], logit[c][:], ACT.Tanh, scale=0.5)
-            a4 = sb([P, PACK, n], F32, "a4_%d" % c, tag="logit%d" % c)
-            both = sb([P, PACK, n], F32, "both%d" % c)
-            res = sb([P, PACK, n], F32, "res%d" % c)
-            for t in range(PACK):
-                gather(a4[:, t, :], a_half[t], n4_sb[:, c0 // 16 : (c0 + n) // 16])
-                nc.vector.tensor_tensor(both[:, t, :], a4[:, t, :], a_half[t][:, c0 : c0 + n], ALU.add)
-                nc.vector.scalar_tensor_tensor(res[:, t, :], th2[:, t, :], 1.0, both[:, t, :], ALU.add, ALU.mult)
-                if t % 2 == 1:
-                    nc.sync.dma_start(out_rows[:, t - 1 : t + 1, c0 : c0 + n], res[:, t - 1 : t + 1, :])
-            o_bf = sb([P, PACK * n], BF16, "o_bf%d" % c)
-            quantize(res[:], o_w[:, c0 : c0 + n], o_s[:, c0 : c0 + n], o_bf[:])
-            nc.sync.dma_start(out_words[:, c0 : c0 + n], o_w[:, c0 : c0 + n].bitcast(I32))
+        a4 = sb([P, PACK, S], F32, "a4", tag="y_n2")
+        a4_homes = ([a4[:, t, :] for t in range(PACK)], [b5[:, 2, :], b5[:, 0, :], b5[:, 3, :], b5[:, 1, :]])
+        both = sb([P, PACK, S], F32, "both", tag="members0")
+        res = sb([P, PACK, S], F32, "res", tag="members1")
+        o_bf = sb([P, PACK * S], BF16, "o_bf", tag="members2")
+        for h in range(2):
+            gate = []
+            for u in range(2):
+                th_t = a_half[u][:, S:].rearrange("p (t b n) -> p t b n", t=2, b=2)
+                nc.scalar.activation(th_t, logit_ps[h, u][:], ACT.Tanh, scale=0.5)
+                bank = psum.tile([P, 2, 2, P], F32, name="gate_ps%d%d" % (h, u), tag="bank%d" % logit_bank[h][u])
+                for tt in range(2):
+                    for jb in range(2):
+                        nc.tensor.transpose(bank[:, tt, jb, :], th_t[:, tt, jb, :], ident[:])
+                gate.append(bank[:].rearrange("p t b n -> p t (b n)"))
+            for c0, n in OUT_CHUNKS[h]:
+                cols = slice(c0, c0 + n)
+                for u in range(2):
+                    pair = slice(2 * u, 2 * u + 2)
+                    for t in range(pair.start, pair.stop):
+                        fetched = a4_homes[h][t][:, cols]
+                        gather(fetched, a_half[t], n4_sb[:, c0 // 16 : (c0 + n) // 16])
+                        nc.vector.tensor_tensor(both[:, t, cols], fetched, a_half[t][:, cols], ALU.add)
+                    nc.vector.scalar_tensor_tensor(
+                        res[:, pair, cols], gate[u][:, :, c0 - H * h : c0 - H * h + n], 1.0, both[:, pair, cols],
+                        ALU.add, ALU.mult,
+                    )
+                    nc.sync.dma_start(out_rows[:, pair, cols], res[:, pair, cols])
+                quantize(res[:, :, cols], o_w[:, cols], o_s[:, cols], o_bf[:, PACK * c0 : PACK * (c0 + n)])
+                nc.sync.dma_start(out_words[:, cols], o_w[:, cols].bitcast(I32))
         for q in range(4):
             queue = nc.scalar if q % 2 == 0 else nc.sync
             queue.dma_start(

from contextlib import ExitStack

import concourse.mybir as mybir
from concourse.masks import make_identity

F32 = mybir.dt.float32
BF16 = mybir.dt.bfloat16
I32 = mybir.dt.int32
U32 = mybir.dt.uint32
U16 = mybir.dt.uint16
U8 = mybir.dt.uint8
FP8X4 = mybir.dt.float8_e4m3fn_x4
FP4X4 = mybir.dt.float4_e2m1fn_x4
ACT = mybir.ActivationFunctionType
ALU = mybir.AluOpType

P = 128
PACK = 4
S = 512
T = 1024
G = 2048
MEMBERS = 4
SPARE = 16
H = S // 2
OUT_CHUNKS = (((0, 256),), ((256, 128), (384, 128)))

FLOPS = 3 * 2 * 512 * 512 * 512


def tile_picked_cdkeytriebglsecmp_none_po_kernel(
    tc, x_words, x_scales, w1_words, w1_scales, gs, gk, d_words, d_scales,
    offs, n1, n2, n3, cand, k1, n4, n5, out_0, out_1, out_2,
):
    nc = tc.nc
    with ExitStack() as ctx:
        lists = ctx.enter_context(tc.tile_pool(name="lists", bufs=1))
        keep = ctx.enter_context(tc.tile_pool(name="keep", bufs=1))
        psum = ctx.enter_context(tc.psum_pool(name="psum", bufs=1))

        def load_list(src, name):
            tile = lists.tile([P, src.shape[1]], U16, name=name)
            nc.sync.dma_start(tile[:], src)
            return tile

        def sb(shape, dtype, name, tag=None):
            return keep.tile(shape, dtype, name=name, tag=tag or name, align_bytes=64)

        def zeroed_bytes(width, name):
            tile = sb([P, width], U8, name)
            nc.vector.memset(tile[:].bitcast(I32), 0)
            return tile

        def load_scale_rows(queue, tile, scales, quadrants):
            for q in quadrants:
                rows = scales[0, 4 * q : 4 * q + 4, :].bitcast(I32)
                queue.dma_start(
                    tile[32 * q : 32 * q + 32, :].bitcast(I32),
                    rows.unsqueeze(0).to_broadcast([8, 4, rows.shape[1]]),
                )

        def deal(dst, src):
            nc.vector.tensor_copy(
                dst[:].rearrange("p (t m) -> p t m", t=PACK),
                src[:].rearrange("p (m t) -> p t m", t=PACK),
            )

        def gather(dst, window, offsets):
            nc.scalar.activation(dst, window[:].indirect(offsets), ACT.Copy)

        def quantize(values, codes, scales, staged):
            nc.vector.tensor_copy(
                staged.rearrange("p (c i t) -> p c t i", i=4, t=PACK),
                values.rearrange("p t (c i) -> p c t i", i=4),
            )
            nc.vector.quantize_mx(out=codes.bitcast(FP8X4), scales=scales, in_=staged)

        xs = sb([P, T], U8, "xs")
        ws = sb([P, S], U8, "ws")
        offs_sb = load_list(offs, "offs_sb")
        load_scale_rows(nc.sync, xs, x_scales, (0, 1))
        load_scale_rows(nc.scalar, xs, x_scales, (2, 3))
        xw = sb([P, T], U32, "xw")
        nc.sync.dma_start(xw[:].bitcast(I32), x_words[0].rearrange("p n t -> p (n t)").bitcast(I32))
        ww = sb([P, 2 * S], U8, "ww")
        nc.sync.dma_start(ww[:].bitcast(I32), w1_words[0].bitcast(I32))
        load_scale_rows(nc.sync, ws, w1_scales, (0, 1, 2, 3))
        n1_sb = load_list(n1, "n1_sb")
        gs_sb = sb([P, PACK], F32, "gs_sb")
        nc.sync.dma_start(gs_sb[:], gs.rearrange("(p t) o -> p (t o)", t=PACK))
        n2_sb = load_list(n2, "n2_sb")
        n3_sb = load_list(n3, "n3_sb")
        gk_sb = sb([P, PACK], F32, "gk_sb")
        nc.sync.dma_start(gk_sb[:], gk.rearrange("(p t) o -> p (t o)", t=PACK))
        k1_sb = load_list(k1, "k1_sb")
        dw = sb([P, G], U32, "dw")
        nc.sync.dma_start(dw[:].bitcast(I32), d_words[0].rearrange("p n t -> p (n t)").bitcast(I32))
        ds = zeroed_bytes(G, "ds")
        for e in range(2):
            nc.sync.dma_start(ds[e:P:16, :].bitcast(I32), d_scales[0, e:16:2, :].bitcast(I32))
        cand_sb = load_list(cand, "cand_sb")
        n5_sb = load_list(n5, "n5_sb")
        n4_sb = load_list(n4, "n4_sb")

        ex = [sb([P, MEMBERS * S + SPARE], F32, "ex%d" % t) for t in range(PACK)]
        a_half = [sb([P, S + (S if t < 2 else SPARE)], F32, "a_half%d" % t) for t in range(PACK)]
        b = [sb([P, S + SPARE], F32, "b%d" % t) for t in range(PACK)]
        key_s = zeroed_bytes(S, "key_s")
        ident = sb([P, P], F32, "ident")
        make_identity(nc, ident[:])

        w_first = sb([P, 2 * P], U8, "w_first")
        ws_first = sb([P, P], U8, "ws_first")
        ww_by_t = ww[:].rearrange("p (m t b) -> p t m b", t=PACK, b=2)
        ws_by_t = ws[:].rearrange("p (m t) -> p t m", t=PACK)
        nc.vector.tensor_copy(w_first[:].rearrange("p (m b) -> p m b", b=2), ww_by_t[:, 0])
        xq_s = sb([P, S], U8, "xq_s")
        nc.vector.tensor_copy(xq_s[:], xs[:].indirect(offs_sb[:]))
        xq_w = sb([P, S], U32, "xq_w")
        for h in range(2):
            nc.vector.tensor_copy(xq_w[:, H * h : H * (h + 1)], xw[:].indirect(offs_sb[:, 16 * h : 16 * (h + 1)]))
            if h == 0:
                nc.vector.tensor_copy(ws_first[:], ws_by_t[:, 0])

        y = [sb([P, 2 * S], F32, "y%d" % t) for t in range(PACK)]
        y_gk = sb([P, PACK, S], F32, "y_gk")

        def project(t, lhs_w, lhs_s, cols, bank_no):
            bank = psum.tile([P, cols.stop - cols.start], F32, name="y_ps%d" % bank_no, tag="bank%d" % bank_no)
            nc.tensor.matmul_mx(
                out=bank[:],
                lhsT=lhs_w.bitcast(FP4X4),
                lhsT_scale=lhs_s,
                rhs=xq_w[:, cols].bitcast(FP8X4),
                rhs_scale=xq_s[:, cols],
                start=True,
                stop=True,
            )
            return bank

        halves = [project(0, w_first[:], ws_first[:], slice(H * h, H * (h + 1)), PACK * h) for h in range(2)]
        for h in range(2):
            nc.scalar.activation(ex[0][:, H * h : H * (h + 1)], halves[h][:], ACT.Exp)
        ws_rest = sb([P, (PACK - 1) * P], U8, "ws_rest")
        nc.vector.tensor_copy(ws_rest[:].rearrange("p (t m) -> p t m", t=PACK - 1), ws_by_t[:, 1:])
        w_rest = sb([P, (PACK - 1) * 2 * P], U8, "w_rest", tag="ws")
        nc.vector.tensor_copy(w_rest[:].rearrange("p (t m b) -> p t m b", t=PACK - 1, b=2), ww_by_t[:, 1:])
        y_ps = [None] + [
            project(t, w_rest[:, 2 * P * (t - 1) : 2 * P * t], ws_rest[:, P * (t - 1) : P * t], slice(0, S), t)
            for t in range(1, PACK)
        ]
        members = [sb([P, MEMBERS * S], F32, "members%d" % t) for t in range(PACK)]
        pairs = sb([P, 2 * S], F32, "pairs")
        total = sb([P, PACK, S], F32, "total")

        def fetch_members(t, pieces=1):
            n = MEMBERS * S // pieces
            for c in range(pieces):
                gather(members[t][:, n * c : n * (c + 1)], ex[t], n1_sb[:, n * c // 16 : n * (c + 1) // 16])

        def member_sums(t, pieces=1):
            n = S // pieces
            view = members[t][:].rearrange("p (j h e) -> p j h e", h=2, e=2)
            pv = pairs[:].rearrange("p (j e) -> p j e", e=2)
            for c in range(pieces):
                js = slice(n * c, n * (c + 1))
                nc.vector.tensor_tensor(pv[:, js], view[:, js, 0, :], view[:, js, 1, :], ALU.add)
                nc.vector.tensor_tensor(total[:, t, js], pv[:, js, 0], pv[:, js, 1], ALU.add)
                nc.vector.tensor_tensor(total[:, t, js], total[:, t, js], ex[t][:, js], ALU.add)

        fetch_members(0)
        for t in range(PACK):
            if t == 0:
                for h in range(2):
                    nc.vector.tensor_copy(y[0][:, H * h : H * (h + 1)], halves[h][:])
            else:
                nc.scalar.activation(ex[t][:, :S], y_ps[t][:], ACT.Exp)
                nc.vector.tensor_copy(y[t][:, :S], y_ps[t][:])
            nc.vector.tensor_scalar(y[t][:, S:], y[t][:, :S], gs_sb[:, t : t + 1], None, ALU.mult)

        key_w_raw = sb([P, S], U32, "key_w_raw", tag="ww")
        nc.vector.tensor_copy(key_w_raw[:], dw[:].indirect(k1_sb[:]))
        key_s_raw = sb([P, S], U8, "key_s_raw", tag="ws")
        nc.vector.tensor_copy(key_s_raw[:], ds[:].indirect(k1_sb[:]))
        key_s_dealt = sb([P, S], U8, "key_s_dealt")
        deal(key_s_dealt, key_s_raw)
        for h in range(2):
            for e in range(2):
                nc.sync.dma_start(
                    key_s[2 * h + e : P : 32, :].bitcast(I32),
                    key_s_dealt[16 * h + e : P : 32, :].bitcast(I32),
                )
        key_w = sb([P, S], U32, "key_w")
        deal(key_w, key_w_raw)

        y2 = sb([P, PACK, S], F32, "y_n2")
        y3 = sb([P, PACK, S], F32, "y_n3")
        diff = sb([P, PACK, S], F32, "diff")
        for t in range(PACK):
            gather(y2[:, t, :], y[t], n2_sb[:])
            gather(y3[:, t, :], y[t], n3_sb[:])
            nc.vector.tensor_scalar(y_gk[:, t, :], y[t][:, :S], gk_sb[:, t : t + 1], 0.5, ALU.mult, ALU.mult)
            nc.vector.tensor_tensor(diff[:, t, :], y2[:, t, :], y3[:, t, :], ALU.subtract)
        member_sums(0)
        th1 = sb([P, PACK, S], F32, "th1", tag="y_n2")
        nc.scalar.activation(th1[:], diff[:], ACT.Tanh, scale=0.5)

        cand_w_raw = sb([P, S], U32, "cand_w_raw", tag="ww")
        nc.vector.tensor_copy(cand_w_raw[:], xw[:].indirect(cand_sb[:]))
        cand_s_raw = sb([P, S], U8, "cand_s_raw", tag="ws")
        nc.vector.tensor_copy(cand_s_raw[:], xs[:].indirect(cand_sb[:]))
        cand_w = sb([P, S], U32, "cand_w")
        deal(cand_w, cand_w_raw)
        cand_s = sb([P, S], U8, "cand_s")
        deal(cand_s, cand_s_raw)

        def product(stat_w, stat_s, mov_w, mov_s, first_bank, dst, factor, name):
            for t in range(PACK):
                bank = psum.tile([P, S], F32, name="%s_ps%d" % (name, t), tag="bank%d" % (first_bank + t))
                nc.tensor.matmul_mx(
                    out=bank[:],
                    lhsT=stat_w[:, P * t : P * (t + 1)].bitcast(FP8X4),
                    lhsT_scale=stat_s[:, P * t : P * (t + 1)],
                    rhs=mov_w[:].bitcast(FP8X4),
                    rhs_scale=mov_s[:],
                    start=True,
                    stop=True,
                )
                nc.vector.tensor_scalar(dst[t][:, :S], bank[:], factor, None, ALU.mult)

        z2 = sb([P, PACK, S], F32, "z2", tag="y_n3")
        nc.vector.scalar_tensor_tensor(z2[:], th1[:], 1.0, y_gk[:], ALU.add, ALU.mult)
        z2_bf = sb([P, PACK * S], BF16, "z2_bf")
        z2_w = sb([P, S], U32, "z2_w")
        z2_s = sb([P, S], U8, "z2_s")
        quantize(z2[:], z2_w[:], z2_s[:], z2_bf[:])
        fetch_members(1)
        member_sums(1)
        product(key_w, key_s, z2_w, z2_s, PACK, b, 0.0625, "b")
        fetch_members(2)
        member_sums(2)
        fetch_members(3, 2)
        member_sums(3, 2)

        logs = sb([P, PACK, S], F32, "logs")
        nc.scalar.activation(logs[:, : PACK - 1, :], total[:, : PACK - 1, :], ACT.Ln)
        nc.scalar.activation(logs[:, PACK - 1, :], total[:, PACK - 1, :], ACT.Ln)
        z = sb([P, PACK, S], F32, "z", tag="diff")
        for t in range(PACK):
            nc.vector.scalar_tensor_tensor(
                z[:, t, :], logs[:, t, :], gs_sb[:, t : t + 1], y[t][:, S:], ALU.mult, ALU.subtract
            )
        z_bf = sb([P, PACK * S], BF16, "z_bf")
        z_w = sb([P, S], U32, "z_w")
        z_s = sb([P, S], U8, "z_s")
        quantize(z[:], z_w[:], z_s[:], z_bf[:])

        b5 = sb([P, PACK, S], F32, "b5", tag="total")
        for t in range(PACK):
            gather(b5[:, t, :], b[t], n5_sb[:])
        product(cand_w, cand_s, z_w, z_s, 0, a_half, 0.03125, "a")
        logit_bank = ((4, 0), (1, 2))
        logit_ps = {}
        for h in range(2):
            for u in range(2):
                bank = psum.tile([P, 2, 2, P], F32, name="logit_ps%d%d" % (h, u), tag="bank%d" % logit_bank[h][u])
                for tt in range(2):
                    t = 2 * u + tt
                    for jb in range(2):
                        js = slice(H * h + P * jb, H * h + P * (jb + 1))
                        for i, term in enumerate((b[t][:, js], b5[:, t, js])):
                            nc.tensor.matmul(
                                bank[:, tt, jb, :], term, ident[:], start=(i == 0), stop=(i == 1), is_transpose=True
                            )
                logit_ps[h, u] = bank

        out_rows = out_0.rearrange("(p t) j -> p t j", t=PACK)
        out_words = out_1[0].rearrange("p n t -> p (n t)").bitcast(I32)
        o_w = sb([P, S], U32, "o_w")
        o_s = sb([P, S], U8, "o_s")
        a4 = sb([P, PACK, S], F32, "a4", tag="y_n2")
        a4_homes = ([a4[:, t, :] for t in range(PACK)], [b5[:, 2, :], b5[:, 0, :], b5[:, 3, :], b5[:, 1, :]])
        both = sb([P, PACK, S], F32, "both", tag="members0")
        res = sb([P, PACK, S], F32, "res", tag="members1")
        o_bf = sb([P, PACK * S], BF16, "o_bf", tag="members2")
        for h in range(2):
            gate = []
            for u in range(2):
                th_t = a_half[u][:, S:].rearrange("p (t b n) -> p t b n", t=2, b=2)
                nc.scalar.activation(th_t, logit_ps[h, u][:], ACT.Tanh, scale=0.5)
                bank = psum.tile([P, 2, 2, P], F32, name="gate_ps%d%d" % (h, u), tag="bank%d" % logit_bank[h][u])
                for tt in range(2):
                    for jb in range(2):
                        nc.tensor.transpose(bank[:, tt, jb, :], th_t[:, tt, jb, :], ident[:])
                gate.append(bank[:].rearrange("p t b n -> p t (b n)"))
            for c0, n in OUT_CHUNKS[h]:
                cols = slice(c0, c0 + n)
                for u in range(2):
                    pair = slice(2 * u, 2 * u + 2)
                    for t in range(pair.start, pair.stop):
                        fetched = a4_homes[h][t][:, cols]
                        gather(fetched, a_half[t], n4_sb[:, c0 // 16 : (c0 + n) // 16])
                        nc.vector.tensor_tensor(both[:, t, cols], fetched, a_half[t][:, cols], ALU.add)
                    nc.vector.scalar_tensor_tensor(
                        res[:, pair, cols], gate[u][:, :, c0 - H * h : c0 - H * h + n], 1.0, both[:, pair, cols],
                        ALU.add, ALU.mult,
                    )
                    nc.sync.dma_start(out_rows[:, pair, cols], res[:, pair, cols])
                quantize(res[:, :, cols], o_w[:, cols], o_s[:, cols], o_bf[:, PACK * c0 : PACK * (c0 + n)])
                nc.sync.dma_start(out_words[:, cols], o_w[:, cols].bitcast(I32))
        for q in range(4):
            queue = nc.scalar if q % 2 == 0 else nc.sync
            queue.dma_start(
                out_2[0, 4 * q : 4 * q + 4, :].bitcast(I32), o_s[32 * q : 32 * q + 4, :].bitcast(I32)
            )
